import numpy as np
import ml_dtypes


def mxq(x, axis, fmt="e4m3"):
    dtype, down = {"e4m3": (ml_dtypes.float8_e4m3fn, 7), "e5m2": (ml_dtypes.float8_e5m2, 14)}[fmt]
    v = np.moveaxis(np.asarray(x, np.float32).astype(ml_dtypes.bfloat16).astype(np.float64), axis, -1)
    blocks = v.reshape(v.shape[:-1] + (-1, 32))
    amax = np.abs(blocks).max(-1, keepdims=True)
    byte = np.maximum(np.where(amax > 0, np.frexp(amax)[1] - 1 + 127, 0) - down, 1)
    scale = np.exp2(byte - 127.0)
    codes = (blocks / scale).astype(np.float32).astype(dtype).astype(np.float64)
    return np.moveaxis((codes * scale).reshape(v.shape), -1, axis)


WIDE = False


def mx_kscale(k):
    if not WIDE:
        return np.ones(k)
    levels = np.array([10, -10, 5, -5, 0])
    if k % 512:
        return np.exp2(np.random.permutation(np.resize(levels, k // 32))).repeat(32)
    a = np.empty((k // 512, 16))
    for p in range(k // 512):
        a[p, :8] = np.random.permutation(np.resize(levels, 8))
        for g in range(8):
            far = levels[np.abs(levels - a[p, g]) >= 10]
            a[p, g + 8] = far[np.random.randint(len(far))]
    return np.exp2(a.ravel()).repeat(32)


def f64(x):
    return np.asarray(x).astype(np.float64)


def striped8(idx):
    return np.asarray(idx).reshape(8, -1, 16).transpose(0, 2, 1).reshape(128, -1).astype(np.uint16)


def unstriped8(offs):
    return offs.reshape(8, 16, -1).transpose(0, 2, 1).reshape(8, -1).astype(np.int64)


def pick8(x, idx, run):
    r = np.arange(len(x))
    return x[r[:, None], idx[r % (8 * run) // run]]


E2M1 = np.array([0.0, 0.5, 1.0, 1.5, 2.0, 3.0, 4.0, 6.0, -0.0, -0.5, -1.0, -1.5, -2.0, -3.0, -4.0, -6.0])


def pack_weight(w, fmt):
    k, n = w.shape
    w = f64(np.asarray(w, np.float32).astype(ml_dtypes.bfloat16)).reshape(k // 32, 32, n)
    amax = np.abs(w).max(1)
    if fmt == "e4m3":
        byte = np.frexp(amax)[1] - 1 + 127 - 7
    else:
        mant, ex = np.frexp(amax / 6.0)
        byte = np.where(mant > 0.5, ex, ex - 1) + 127
    byte = np.clip(np.where(amax > 0, byte, 1), 1, 254)
    scaled = (w * np.exp2(127.0 - byte)[:, None, :]).reshape(k, n).astype(np.float32)
    by_word = np.ascontiguousarray(scaled.reshape(k // 512, 128, 4, n).transpose(0, 1, 3, 2))
    if fmt == "e4m3":
        words = by_word.astype(ml_dtypes.float8_e4m3fn).view(np.uint8)
    else:
        c = by_word.astype(ml_dtypes.float4_e2m1fn).view(np.uint8) & 0xF
        words = (c[..., 0::2] | (c[..., 1::2] << 4)).reshape(k // 512, 128, 2 * n)
    return np.ascontiguousarray(words), np.ascontiguousarray(byte.astype(np.uint8).reshape(k // 512, 16, n))


def unpack_weight(words, scales, fmt):
    g, _, n = scales.shape
    words = np.ascontiguousarray(words).reshape(g, 128, n, -1)
    if fmt == "e4m3":
        vals = words.view(ml_dtypes.float8_e4m3fn).astype(np.float64)
    else:
        nib = np.empty((g, 128, n, 4), np.uint8)
        nib[..., 0::2] = words & 0xF
        nib[..., 1::2] = words >> 4
        vals = E2M1[nib]
    vals = vals * np.repeat(np.exp2(scales.astype(np.float64) - 127.0), 8, axis=1)[..., None]
    return vals.transpose(0, 1, 3, 2).reshape(g * 512, n)


def sgn(shape):
    return np.random.uniform(0.5, 2.0, shape) * np.where(np.random.standard_normal(shape) < 0, -1.0, 1.0)


D, T, Z, I, Q, E = 512, 1024, 1024, 512, 512, 256


def setup_inputs():
    n = np.random.standard_normal
    idx = np.stack([np.random.permutation(T)[:I] for _ in range(8)])
    idx2 = np.stack([np.random.permutation(T)[:I] for _ in range(8)])
    idx3 = np.stack([np.random.permutation(Z)[:I] for _ in range(8)])
    idx4 = np.stack([np.random.permutation(Z)[:I] for _ in range(8)])
    fd = mx_kscale(D)
    fq = mx_kscale(Q)
    cachep = pack_weight(n((D, T)) / fd[:, None], "e2m1")
    mixp = pack_weight(n((Q, E)) * 1.0 / np.sqrt(Q) / fq[:, None], "e4m3")
    return {
        "query": (n((D, Q)) * 1.0 / np.sqrt(D) * fd[:, None]).astype(np.float32),
        "cache_words": cachep[0],
        "cache_scales": cachep[1],
        "sa": (sgn((Q, 1))).astype(np.float32),
        "rowf": (np.random.uniform(0.5, 2.0, (Q, 1)) * fq[:, None]).astype(np.float32),
        "mix_words": mixp[0],
        "mix_scales": mixp[1],
        "offs": striped8(idx),
        "offs2": striped8(idx2),
        "offs3": striped8(idx3),
        "offs4": striped8(idx4),
    }


def reference(query, cache_words, cache_scales, sa, rowf, mix_words, mix_scales, offs, offs2, offs3, offs4):
    idx = unstriped8(offs)
    idx2 = unstriped8(offs2)
    idx3 = unstriped8(offs3)
    idx4 = unstriped8(offs4)
    cacheu = unpack_weight(cache_words, cache_scales, "e2m1")
    mixu = unpack_weight(mix_words, mix_scales, "e4m3")
    queryq = mxq(f64(query), 0, "e4m3")
    a = queryq.T @ cacheu
    w = pick8(a, idx, 64) * f64(sa)
    g = w - pick8(a, idx2, 64)
    gw = g * f64(rowf)
    gwq = mxq(gw, 0, "e4m3")
    o1 = mixu.T @ gwq
    pa = np.zeros((E, Z))
    pa[np.arange(E)[:, None], idx3[np.arange(E) % 128 // 16]] = o1
    pb = np.zeros((E, Z))
    pb[np.arange(E)[:, None], idx4[np.arange(E) % 128 // 16]] = o1
    y = pa - pb
    return y

@@ -1,0 +1,201 @@
+from contextlib import ExitStack
+
+import concourse.mybir as mybir
+
+D, T, Z, I, Q, E = 512, 1024, 1024, 512, 512, 256
+FLOPS = 2 * D * Q * T + 2 * Q * E * I
+
+F32 = mybir.dt.float32
+BF16 = mybir.dt.bfloat16
+I32 = mybir.dt.int32
+U32 = mybir.dt.uint32
+U16 = mybir.dt.uint16
+U8 = mybir.dt.uint8
+FP8X4 = mybir.dt.float8_e4m3fn_x4
+FP4X4 = mybir.dt.float4_e2m1fn_x4
+COPY = mybir.ActivationFunctionType.Copy
+MULT = mybir.AluOpType.mult
+SUB = mybir.AluOpType.subtract
+
+P = 128
+PACK = 4
+BANK = 512
+HALF = I // 2
+PIECE = 128
+GROUP = 16
+STORE = 256
+
+
+def tile_attend_leadscaled_one_twoposts_kernel(
+    tc, query, cache_words, cache_scales, sa, rowf, mix_words, mix_scales, offs, offs2, offs3, offs4, out
+):
+    nc = tc.nc
+    with ExitStack() as ctx:
+        keep = ctx.enter_context(tc.tile_pool(name="keep", bufs=1))
+        psum = ctx.enter_context(tc.psum_pool(name="psum", bufs=8))
+
+        def listed(tile, first, count):
+            return tile[:, first // GROUP : (first + count) // GROUP]
+
+        cache_plane = keep.tile([P, T], U8, align_bytes=64)
+        mix_plane = keep.tile([P, E], U8, align_bytes=64)
+        nc.gpsimd.memset(cache_plane[:].bitcast(I32), 0)
+        nc.gpsimd.memset(mix_plane[:].bitcast(I32), 0)
+
+        rowf_sb = keep.tile([P, PACK], F32)
+        sa_sb = keep.tile([P, PACK], F32)
+
+        nc.scalar.dma_start(rowf_sb[:], rowf.rearrange("(p r) o -> p (r o)", r=PACK))
+        by_place = query.rearrange("(p j) q -> p j q", j=PACK)
+        raw = []
+        for h in range(2):
+            part = keep.tile([P, PACK, Q // 2], F32, name="raw%d" % h)
+            nc.sync.dma_start(part[:], by_place[:, :, h * (Q // 2) : (h + 1) * (Q // 2)])
+            raw.append(part)
+        for quad in range(4):
+            nc.sync.dma_start(
+                cache_plane[32 * quad : 32 * quad + 4, :].bitcast(I32),
+                cache_scales[0, 4 * quad : 4 * quad + 4, :].bitcast(I32),
+            )
+        cache_sb = keep.tile([P, 2 * T], U8, align_bytes=64)
+        nc.sync.dma_start(cache_sb[:].bitcast(I32), cache_words[0].bitcast(I32))
+        offs_sb = keep.tile([P, I // GROUP], U16)
+        offs2_sb = keep.tile([P, I // GROUP], U16)
+        offs3_sb = keep.tile([P, I // GROUP], U16)
+        offs4_sb = keep.tile([P, I // GROUP], U16)
+        nc.sync.dma_start(offs_sb[:], offs)
+        nc.sync.dma_start(sa_sb[:], sa.rearrange("(p r) o -> p (r o)", r=PACK))
+        nc.sync.dma_start(offs2_sb[:], offs2)
+        mix_sb = keep.tile([P, E], U32, align_bytes=64)
+        nc.sync.dma_start(mix_sb[:].bitcast(I32), mix_words[0].rearrange("p e r -> p (e r)").bitcast(I32))
+        nc.sync.dma_start(offs3_sb[:], offs3)
+        nc.sync.dma_start(offs4_sb[:], offs4)
+        for quad in range(4):
+            nc.sync.dma_start(
+                mix_plane[32 * quad : 32 * quad + 4, :].bitcast(I32),
+                mix_scales[0, 4 * quad : 4 * quad + 4, :].bitcast(I32),
+            )
+
+        minus_rowf = keep.tile([P, PACK], F32)
+        nc.vector.tensor_scalar(minus_rowf[:], rowf_sb[:], -1.0, None, MULT)
+
+        pages = [[keep.tile([P, Z], F32, name="page%d%d" % (e, k)) for k in range(2)] for e in range(E // P)]
+        for e in range(E // P):
+            for k in range(2):
+                engine = nc.gpsimd if (e, k) == (1, 1) else nc.vector
+                engine.memset(pages[e][k][:].bitcast(I32), 0)
+
+        dealt = [keep.tile([P, 2, P, PACK], BF16, name="dealt%d" % u, align_bytes=64) for u in range(2)]
+        for h in range(2):
+            src = raw[h][:].rearrange("p j (s r) -> p s j r", r=PACK)
+            for u in range(2):
+                dst = dealt[u][:, :, h * (P // 2) : (h + 1) * (P // 2), :].rearrange("p r s j -> p s j r")
+                if u == 0:
+                    nc.vector.tensor_copy(dst, src[:, :, :, 0:2])
+                else:
+                    nc.scalar.activation(dst, src[:, :, :, 2:4], COPY)
+        q_codes = [keep.tile([P, P], U32, name="q_codes%d" % r, tag="q_codes%d" % r, align_bytes=64) for r in range(PACK)]
+        q_plane = [keep.tile([P, P], U8, name="q_plane%d" % r, align_bytes=64) for r in range(PACK)]
+        for r in range(PACK):
+            nc.vector.quantize_mx(
+                out=q_codes[r][:].bitcast(FP8X4),
+                scales=q_plane[r][:],
+                in_=dealt[r // 2][:, r % 2, :, :].rearrange("p s j -> p (s j)"),
+            )
+
+        scores = [keep.tile([P, T], F32, name="scores%d" % r) for r in range(PACK)]
+        minus_g = keep.tile([P, PACK, HALF], F32, name="minus_g0", tag="minus_g")
+
+        def look_up(r, half, w, minus_g):
+            nc.scalar.activation(
+                w, scores[r][:].indirect(listed(offs_sb, half * HALF, HALF)), COPY, scale=sa_sb[:, r : r + 1]
+            )
+            second = scores[r][:].indirect(listed(offs2_sb, half * HALF, HALF))
+            if (r, half) == (PACK - 1, 0):
+                fetched = keep.tile([P, HALF], F32, name="fetched")
+                nc.vector.tensor_copy(fetched[:], second)
+                for piece in range(HALF // PIECE):
+                    cols = slice(piece * PIECE, (piece + 1) * PIECE)
+                    nc.vector.tensor_tensor(minus_g[:, r, cols], fetched[:, cols], w[:, cols], SUB)
+            else:
+                nc.vector.tensor_tensor(minus_g[:, r, :], second, w, SUB)
+
+        for r in range(PACK):
+            for b in range(T // BANK):
+                bank = psum.tile([P, BANK], F32, name="bank", tag="bank")
+                nc.tensor.matmul_mx(
+                    out=bank[:],
+                    lhsT=q_codes[r][:].bitcast(FP8X4),
+                    lhsT_scale=q_plane[r][:],
+                    rhs=cache_sb[:, 2 * BANK * b : 2 * BANK * (b + 1)].bitcast(FP4X4),
+                    rhs_scale=cache_plane[:, BANK * b : BANK * (b + 1)],
+                    start=True,
+                    stop=True,
+                )
+                if b == 0:
+                    nc.vector.tensor_copy(scores[r][:, BANK * b : BANK * (b + 1)], bank[:])
+                else:
+                    nc.scalar.copy(scores[r][:, BANK * b : BANK * (b + 1)], bank[:])
+            w_first = keep.tile([P, HALF], F32, name="w_first", tag="w%d" % r)
+            look_up(r, 0, w_first[:], minus_g)
+
+        mixed = [keep.tile([P, I], F32, name="mixed%d" % e) for e in range(E // P)]
+
+        def mix_piece(piece, minus_g):
+            local = (piece * PIECE) % HALF
+            woven = keep.tile([P, PIECE, PACK], BF16, name="woven", tag="woven", align_bytes=64)
+            nc.vector.tensor_tensor(
+                woven[:].rearrange("p (c i) r -> p c r i", i=4),
+                minus_g[:, :, local : local + PIECE].rearrange("p r (c i) -> p c r i", i=4),
+                minus_rowf[:].unsqueeze(1).unsqueeze(3).to_broadcast([P, PIECE // 4, PACK, 4]),
+                MULT,
+            )
+            g_codes = keep.tile([P, PIECE], U32, name="g_codes%d" % piece, align_bytes=64)
+            g_plane = keep.tile([P, PIECE], U8, name="g_plane%d" % piece, align_bytes=64)
+            nc.vector.quantize_mx(
+                out=g_codes[:].bitcast(FP8X4), scales=g_plane[:], in_=woven[:].rearrange("p i r -> p (i r)")
+            )
+            for e in range(E // P):
+                bank = psum.tile([P, BANK], F32, name="bank", tag="bank")
+                nc.tensor.matmul_mx(
+                    out=bank[:, 0:PIECE],
+                    lhsT=mix_sb[:, e * P : (e + 1) * P].bitcast(FP8X4),
+                    lhsT_scale=mix_plane[:, e * P : (e + 1) * P],
+                    rhs=g_codes[:].bitcast(FP8X4),
+                    rhs_scale=g_plane[:],
+                    start=True,
+                    stop=True,
+                )
+                if piece == 0 and e == 0:
+                    nc.scalar.copy(mixed[e][:, piece * PIECE : (piece + 1) * PIECE], bank[:, 0:PIECE])
+                else:
+                    nc.vector.tensor_copy(mixed[e][:, piece * PIECE : (piece + 1) * PIECE], bank[:, 0:PIECE])
+
+        def post(e, first, count):
+            for k, lists in enumerate((offs3_sb, offs4_sb)):
+                nc.scalar.activation(
+                    pages[e][k][:].indirect(listed(lists, first, count)), mixed[e][:, first : first + count], COPY
+                )
+
+        def hand_out(e):
+            for c in range(Z // STORE):
+                cols = slice(c * STORE, (c + 1) * STORE)
+                page = keep.tile([P, STORE], F32, name="result%d%d" % (e, c))
+                nc.vector.tensor_tensor(page[:], pages[e][0][:, cols], pages[e][1][:, cols], SUB)
+                nc.sync.dma_start(out[e * P : (e + 1) * P, cols], page[:])
+
+        for piece in range(2):
+            mix_piece(piece, minus_g)
+        w_second = keep.tile([P, PACK, HALF], F32, name="w_second", tag="q_codes3", align_bytes=64)
+        minus_g_second = keep.tile([P, PACK, HALF], F32, name="minus_g1", tag="minus_g")
+        for r in range(PACK):
+            look_up(r, 1, w_second[:, r, :], minus_g_second)
+        for piece in range(2):
+            for e in range(E // P):
+                post(e, piece * PIECE, PIECE)
+        for piece in range(2, 4):
+            mix_piece(piece, minus_g_second)
+            post(0, piece * PIECE, PIECE)
+        hand_out(0)
+        post(1, HALF, HALF)
+        hand_out(1)

@@ -24,6 +24,7 @@ HALF = I // 2
 PIECE = 128
 GROUP = 16
 STORE = 256
+Q_PARTS = ((0, 384), (384, 512))
 
 
 def tile_attend_leadscaled_one_twoposts_kernel(
@@ -48,9 +49,9 @@ def tile_attend_leadscaled_one_twoposts_kernel(
         nc.scalar.dma_start(rowf_sb[:], rowf.rearrange("(p r) o -> p (r o)", r=PACK))
         by_place = query.rearrange("(p j) q -> p j q", j=PACK)
         raw = []
-        for h in range(2):
-            part = keep.tile([P, PACK, Q // 2], F32, name="raw%d" % h)
-            nc.sync.dma_start(part[:], by_place[:, :, h * (Q // 2) : (h + 1) * (Q // 2)])
+        for h, (first, last) in enumerate(Q_PARTS):
+            part = keep.tile([P, PACK, last - first], F32, name="raw%d" % h)
+            nc.sync.dma_start(part[:], by_place[:, :, first:last])
             raw.append(part)
         for quad in range(4):
             nc.sync.dma_start(
@@ -86,10 +87,10 @@ def tile_attend_leadscaled_one_twoposts_kernel(
                 engine.memset(pages[e][k][:].bitcast(I32), 0)
 
         dealt = [keep.tile([P, 2, P, PACK], BF16, name="dealt%d" % u, align_bytes=64) for u in range(2)]
-        for h in range(2):
+        for h, (first, last) in enumerate(Q_PARTS):
             src = raw[h][:].rearrange("p j (s r) -> p s j r", r=PACK)
             for u in range(2):
-                dst = dealt[u][:, :, h * (P // 2) : (h + 1) * (P // 2), :].rearrange("p r s j -> p s j r")
+                dst = dealt[u][:, :, first // PACK : last // PACK, :].rearrange("p r s j -> p s j r")
                 if u == 0:
                     nc.vector.tensor_copy(dst, src[:, :, :, 0:2])
                 else:
@@ -110,15 +111,14 @@ def tile_attend_leadscaled_one_twoposts_kernel(
             nc.scalar.activation(
                 w, scores[r][:].indirect(listed(offs_sb, half * HALF, HALF)), COPY, scale=sa_sb[:, r : r + 1]
             )
-            second = scores[r][:].indirect(listed(offs2_sb, half * HALF, HALF))
-            if (r, half) == (PACK - 1, 0):
-                fetched = keep.tile([P, HALF], F32, name="fetched")
-                nc.vector.tensor_copy(fetched[:], second)
-                for piece in range(HALF // PIECE):
-                    cols = slice(piece * PIECE, (piece + 1) * PIECE)
-                    nc.vector.tensor_tensor(minus_g[:, r, cols], fetched[:, cols], w[:, cols], SUB)
-            else:
-                nc.vector.tensor_tensor(minus_g[:, r, :], second, w, SUB)
+            nc.vector.tensor_tensor(
+                minus_g[:, r, :], scores[r][:].indirect(listed(offs2_sb, half * HALF, HALF)), w, SUB
+            )
+
+        def look_up_first(r):
+            tag = "q_codes%d" % (r + 1) if r in (1, 2) else "w%d" % r
+            w_first = keep.tile([P, HALF], F32, name="w_first", tag=tag, align_bytes=64)
+            look_up(r, 0, w_first[:], minus_g)
 
         for r in range(PACK):
             for b in range(T // BANK):
@@ -132,12 +132,13 @@ def tile_attend_leadscaled_one_twoposts_kernel(
                     start=True,
                     stop=True,
                 )
-                if b == 0:
-                    nc.vector.tensor_copy(scores[r][:, BANK * b : BANK * (b + 1)], bank[:])
-                else:
+                if b == 0 and r != 1:
                     nc.scalar.copy(scores[r][:, BANK * b : BANK * (b + 1)], bank[:])
-            w_first = keep.tile([P, HALF], F32, name="w_first", tag="w%d" % r)
-            look_up(r, 0, w_first[:], minus_g)
+                else:
+                    nc.vector.tensor_copy(scores[r][:, BANK * b : BANK * (b + 1)], bank[:])
+            if r > 0:
+                look_up_first(r - 1)
+        look_up_first(PACK - 1)
 
         mixed = [keep.tile([P, I], F32, name="mixed%d" % e) for e in range(E // P)]
 

@@ -23,6 +23,7 @@ BANK = 512
 HALF = I // 2
 PIECE = 128
 GROUP = 16
+LEAD = 64
 STORE = 256
 Q_PARTS = ((0, 384), (384, 512))
 
@@ -96,7 +97,7 @@ def tile_attend_leadscaled_one_twoposts_kernel(
                 else:
                     nc.scalar.activation(dst, src[:, :, :, 2:4], COPY)
         q_codes = [keep.tile([P, P], U32, name="q_codes%d" % r, tag="q_codes%d" % r, align_bytes=64) for r in range(PACK)]
-        q_plane = [keep.tile([P, P], U8, name="q_plane%d" % r, align_bytes=64) for r in range(PACK)]
+        q_plane = [keep.tile([P, P], U8, name="q_plane%d" % r, tag="q_plane%d" % r, align_bytes=64) for r in range(PACK)]
         for r in range(PACK):
             nc.vector.quantize_mx(
                 out=q_codes[r][:].bitcast(FP8X4),
@@ -107,18 +108,22 @@ def tile_attend_leadscaled_one_twoposts_kernel(
         scores = [keep.tile([P, T], F32, name="scores%d" % r) for r in range(PACK)]
         minus_g = keep.tile([P, PACK, HALF], F32, name="minus_g0", tag="minus_g")
 
-        def look_up(r, half, w, minus_g):
+        def fetch_scaled(r, half, w):
             nc.scalar.activation(
                 w, scores[r][:].indirect(listed(offs_sb, half * HALF, HALF)), COPY, scale=sa_sb[:, r : r + 1]
             )
+
+        def fetch_less(r, half, w, minus_g):
             nc.vector.tensor_tensor(
                 minus_g[:, r, :], scores[r][:].indirect(listed(offs2_sb, half * HALF, HALF)), w, SUB
             )
 
-        def look_up_first(r):
-            tag = "q_codes%d" % (r + 1) if r in (1, 2) else "w%d" % r
-            w_first = keep.tile([P, HALF], F32, name="w_first", tag=tag, align_bytes=64)
-            look_up(r, 0, w_first[:], minus_g)
+        w_first = []
+
+        def fetch_first(r):
+            tag = {1: "q_codes3", 2: "q_plane3"}.get(r, "w%d" % r)
+            w_first.append(keep.tile([P, HALF], F32, name="w_first", tag=tag, align_bytes=64))
+            fetch_scaled(r, 0, w_first[r][:])
 
         for r in range(PACK):
             for b in range(T // BANK):
@@ -136,46 +141,74 @@ def tile_attend_leadscaled_one_twoposts_kernel(
                     nc.scalar.copy(scores[r][:, BANK * b : BANK * (b + 1)], bank[:])
                 else:
                     nc.vector.tensor_copy(scores[r][:, BANK * b : BANK * (b + 1)], bank[:])
+            if r > 1:
+                fetch_less(r - 2, 0, w_first[r - 2][:], minus_g)
             if r > 0:
-                look_up_first(r - 1)
-        look_up_first(PACK - 1)
+                fetch_first(r - 1)
+        fetch_first(PACK - 1)
+        for r in range(PACK - 2, PACK):
+            fetch_less(r, 0, w_first[r][:], minus_g)
 
-        mixed = [keep.tile([P, I], F32, name="mixed%d" % e) for e in range(E // P)]
+        mixed = keep.tile([P, E // P, I], F32)
+
+        def weave(woven, minus_g, local, first, count):
+            nc.vector.tensor_tensor(
+                woven[:, first : first + count, :].rearrange("p (c i) r -> p c r i", i=4),
+                minus_g[:, :, local + first : local + first + count].rearrange("p r (c i) -> p c r i", i=4),
+                minus_rowf[:].unsqueeze(1).unsqueeze(3).to_broadcast([P, count // 4, PACK, 4]),
+                MULT,
+            )
 
         def mix_piece(piece, minus_g):
             local = (piece * PIECE) % HALF
-            woven = keep.tile([P, PIECE, PACK], BF16, name="woven", tag="woven", align_bytes=64)
-            nc.vector.tensor_tensor(
-                woven[:].rearrange("p (c i) r -> p c r i", i=4),
-                minus_g[:, :, local : local + PIECE].rearrange("p r (c i) -> p c r i", i=4),
-                minus_rowf[:].unsqueeze(1).unsqueeze(3).to_broadcast([P, PIECE // 4, PACK, 4]),
-                MULT,
-            )
+            slots = slice(piece * PIECE, (piece + 1) * PIECE)
+            woven = keep.tile([P, PIECE, PACK], BF16, name="woven%d" % piece, align_bytes=64)
+            steps = 1 if piece == 2 else 2
+            for step in range(steps):
+                weave(woven, minus_g, local, step * PIECE // steps, PIECE // steps)
             g_codes = keep.tile([P, PIECE], U32, name="g_codes%d" % piece, align_bytes=64)
             g_plane = keep.tile([P, PIECE], U8, name="g_plane%d" % piece, align_bytes=64)
-            nc.vector.quantize_mx(
-                out=g_codes[:].bitcast(FP8X4), scales=g_plane[:], in_=woven[:].rearrange("p i r -> p (i r)")
-            )
-            for e in range(E // P):
-                bank = psum.tile([P, BANK], F32, name="bank", tag="bank")
+            calls = 2 if piece == 0 else 1
+            for call in range(calls):
+                part = slice(call * PIECE // calls, (call + 1) * PIECE // calls)
+                nc.vector.quantize_mx(
+                    out=g_codes[:, part].bitcast(FP8X4),
+                    scales=g_plane[:, part],
+                    in_=woven[:, part, :].rearrange("p i r -> p (i r)"),
+                )
+
+            def mix(target, e, part=slice(0, PIECE)):
                 nc.tensor.matmul_mx(
-                    out=bank[:, 0:PIECE],
+                    out=target,
                     lhsT=mix_sb[:, e * P : (e + 1) * P].bitcast(FP8X4),
                     lhsT_scale=mix_plane[:, e * P : (e + 1) * P],
-                    rhs=g_codes[:].bitcast(FP8X4),
-                    rhs_scale=g_plane[:],
+                    rhs=g_codes[:, part].bitcast(FP8X4),
+                    rhs_scale=g_plane[:, part],
                     start=True,
                     stop=True,
                 )
-                if piece == 0 and e == 0:
-                    nc.scalar.copy(mixed[e][:, piece * PIECE : (piece + 1) * PIECE], bank[:, 0:PIECE])
-                else:
-                    nc.vector.tensor_copy(mixed[e][:, piece * PIECE : (piece + 1) * PIECE], bank[:, 0:PIECE])
+
+            if piece == 0:
+                for e, part in ((0, slice(0, LEAD)), (0, slice(LEAD, PIECE)), (1, slots)):
+                    bank = psum.tile([P, BANK], F32, name="bank", tag="bank")
+                    width = part.stop - part.start
+                    mix(bank[:, 0:width], e, part)
+                    if part.stop == LEAD:
+                        nc.scalar.copy(mixed[:, e, part], bank[:, 0:width])
+                    else:
+                        nc.vector.tensor_copy(mixed[:, e, part], bank[:, 0:width])
+            else:
+                bank = psum.tile([P, BANK], F32, name="bank", tag="bank")
+                for e in range(E // P):
+                    mix(bank[:, e * PIECE : (e + 1) * PIECE], e)
+                nc.vector.tensor_copy(
+                    mixed[:, :, slots], bank[:, 0 : 2 * PIECE].rearrange("p (e i) -> p e i", e=E // P)
+                )
 
         def post(e, first, count):
             for k, lists in enumerate((offs3_sb, offs4_sb)):
                 nc.scalar.activation(
-                    pages[e][k][:].indirect(listed(lists, first, count)), mixed[e][:, first : first + count], COPY
+                    pages[e][k][:].indirect(listed(lists, first, count)), mixed[:, e, first : first + count], COPY
                 )
 
         def hand_out(e):
@@ -190,10 +223,13 @@ def tile_attend_leadscaled_one_twoposts_kernel(
         w_second = keep.tile([P, PACK, HALF], F32, name="w_second", tag="q_codes3", align_bytes=64)
         minus_g_second = keep.tile([P, PACK, HALF], F32, name="minus_g1", tag="minus_g")
         for r in range(PACK):
-            look_up(r, 1, w_second[:, r, :], minus_g_second)
-        for piece in range(2):
-            for e in range(E // P):
-                post(e, piece * PIECE, PIECE)
+            fetch_scaled(r, 1, w_second[:, r, :])
+            fetch_less(r, 1, w_second[:, r, :], minus_g_second)
+        post(0, 0, LEAD)
+        post(0, LEAD, PIECE - LEAD)
+        post(1, 0, PIECE)
+        for e in range(E // P):
+            post(e, PIECE, PIECE)
         for piece in range(2, 4):
             mix_piece(piece, minus_g_second)
             post(0, piece * PIECE, PIECE)

from contextlib import ExitStack

import concourse.mybir as mybir

D, T, Z, I, Q, E = 512, 1024, 1024, 512, 512, 256
FLOPS = 2 * D * Q * T + 2 * Q * E * I

F32 = mybir.dt.float32
BF16 = mybir.dt.bfloat16
I32 = mybir.dt.int32
U32 = mybir.dt.uint32
U16 = mybir.dt.uint16
U8 = mybir.dt.uint8
FP8X4 = mybir.dt.float8_e4m3fn_x4
FP4X4 = mybir.dt.float4_e2m1fn_x4
COPY = mybir.ActivationFunctionType.Copy
MULT = mybir.AluOpType.mult
SUB = mybir.AluOpType.subtract

P = 128
PACK = 4
BANK = 512
HALF = I // 2
PIECE = 128
GROUP = 16
LEAD = 64
STORE = 256
Q_PARTS = ((0, 384), (384, 512))


def tile_attend_leadscaled_one_twoposts_kernel(
    tc, query, cache_words, cache_scales, sa, rowf, mix_words, mix_scales, offs, offs2, offs3, offs4, out
):
    nc = tc.nc
    with ExitStack() as ctx:
        keep = ctx.enter_context(tc.tile_pool(name="keep", bufs=1))
        psum = ctx.enter_context(tc.psum_pool(name="psum", bufs=8))

        def listed(tile, first, count):
            return tile[:, first // GROUP : (first + count) // GROUP]

        cache_plane = keep.tile([P, T], U8, align_bytes=64)
        mix_plane = keep.tile([P, E], U8, align_bytes=64)
        nc.gpsimd.memset(cache_plane[:].bitcast(I32), 0)
        nc.gpsimd.memset(mix_plane[:].bitcast(I32), 0)

        rowf_sb = keep.tile([P, PACK], F32)
        sa_sb = keep.tile([P, PACK], F32)

        nc.scalar.dma_start(rowf_sb[:], rowf.rearrange("(p r) o -> p (r o)", r=PACK))
        by_place = query.rearrange("(p j) q -> p j q", j=PACK)
        raw = []
        for h, (first, last) in enumerate(Q_PARTS):
            part = keep.tile([P, PACK, last - first], F32, name="raw%d" % h)
            nc.sync.dma_start(part[:], by_place[:, :, first:last])
            raw.append(part)
        for quad in range(4):
            nc.sync.dma_start(
                cache_plane[32 * quad : 32 * quad + 4, :].bitcast(I32),
                cache_scales[0, 4 * quad : 4 * quad + 4, :].bitcast(I32),
            )
        cache_sb = keep.tile([P, 2 * T], U8, align_bytes=64)
        nc.sync.dma_start(cache_sb[:].bitcast(I32), cache_words[0].bitcast(I32))
        offs_sb = keep.tile([P, I // GROUP], U16)
        offs2_sb = keep.tile([P, I // GROUP], U16)
        offs3_sb = keep.tile([P, I // GROUP], U16)
        offs4_sb = keep.tile([P, I // GROUP], U16)
        nc.sync.dma_start(offs_sb[:], offs)
        nc.sync.dma_start(sa_sb[:], sa.rearrange("(p r) o -> p (r o)", r=PACK))
        nc.sync.dma_start(offs2_sb[:], offs2)
        mix_sb = keep.tile([P, E], U32, align_bytes=64)
        nc.sync.dma_start(mix_sb[:].bitcast(I32), mix_words[0].rearrange("p e r -> p (e r)").bitcast(I32))
        nc.sync.dma_start(offs3_sb[:], offs3)
        nc.sync.dma_start(offs4_sb[:], offs4)
        for quad in range(4):
            nc.sync.dma_start(
                mix_plane[32 * quad : 32 * quad + 4, :].bitcast(I32),
                mix_scales[0, 4 * quad : 4 * quad + 4, :].bitcast(I32),
            )

        minus_rowf = keep.tile([P, PACK], F32)
        nc.vector.tensor_scalar(minus_rowf[:], rowf_sb[:], -1.0, None, MULT)

        pages = [[keep.tile([P, Z], F32, name="page%d%d" % (e, k)) for k in range(2)] for e in range(E // P)]
        for e in range(E // P):
            for k in range(2):
                engine = nc.gpsimd if (e, k) == (1, 1) else nc.vector
                engine.memset(pages[e][k][:].bitcast(I32), 0)

        dealt = [keep.tile([P, 2, P, PACK], BF16, name="dealt%d" % u, align_bytes=64) for u in range(2)]
        for h, (first, last) in enumerate(Q_PARTS):
            src = raw[h][:].rearrange("p j (s r) -> p s j r", r=PACK)
            for u in range(2):
                dst = dealt[u][:, :, first // PACK : last // PACK, :].rearrange("p r s j -> p s j r")
                if u == 0:
                    nc.vector.tensor_copy(dst, src[:, :, :, 0:2])
                else:
                    nc.scalar.activation(dst, src[:, :, :, 2:4], COPY)
        q_codes = [keep.tile([P, P], U32, name="q_codes%d" % r, tag="q_codes%d" % r, align_bytes=64) for r in range(PACK)]
        q_plane = [keep.tile([P, P], U8, name="q_plane%d" % r, tag="q_plane%d" % r, align_bytes=64) for r in range(PACK)]
        for r in range(PACK):
            nc.vector.quantize_mx(
                out=q_codes[r][:].bitcast(FP8X4),
                scales=q_plane[r][:],
                in_=dealt[r // 2][:, r % 2, :, :].rearrange("p s j -> p (s j)"),
            )

        scores = [keep.tile([P, T], F32, name="scores%d" % r) for r in range(PACK)]
        minus_g = keep.tile([P, PACK, HALF], F32, name="minus_g0", tag="minus_g")

        def fetch_scaled(r, half, w):
            nc.scalar.activation(
                w, scores[r][:].indirect(listed(offs_sb, half * HALF, HALF)), COPY, scale=sa_sb[:, r : r + 1]
            )

        def fetch_less(r, half, w, minus_g):
            nc.vector.tensor_tensor(
                minus_g[:, r, :], scores[r][:].indirect(listed(offs2_sb, half * HALF, HALF)), w, SUB
            )

        w_first = []

        def fetch_first(r):
            tag = {1: "q_codes3", 2: "q_plane3"}.get(r, "w%d" % r)
            w_first.append(keep.tile([P, HALF], F32, name="w_first", tag=tag, align_bytes=64))
            fetch_scaled(r, 0, w_first[r][:])

        for r in range(PACK):
            for b in range(T // BANK):
                bank = psum.tile([P, BANK], F32, name="bank", tag="bank")
                nc.tensor.matmul_mx(
                    out=bank[:],
                    lhsT=q_codes[r][:].bitcast(FP8X4),
                    lhsT_scale=q_plane[r][:],
                    rhs=cache_sb[:, 2 * BANK * b : 2 * BANK * (b + 1)].bitcast(FP4X4),
                    rhs_scale=cache_plane[:, BANK * b : BANK * (b + 1)],
                    start=True,
                    stop=True,
                )
                if b == 0 and r != 1:
                    nc.scalar.copy(scores[r][:, BANK * b : BANK * (b + 1)], bank[:])
                else:
                    nc.vector.tensor_copy(scores[r][:, BANK * b : BANK * (b + 1)], bank[:])
            if r > 1:
                fetch_less(r - 2, 0, w_first[r - 2][:], minus_g)
            if r > 0:
                fetch_first(r - 1)
        fetch_first(PACK - 1)
        for r in range(PACK - 2, PACK):
            fetch_less(r, 0, w_first[r][:], minus_g)

        mixed = keep.tile([P, E // P, I], F32)

        def weave(woven, minus_g, local, first, count):
            nc.vector.tensor_tensor(
                woven[:, first : first + count, :].rearrange("p (c i) r -> p c r i", i=4),
                minus_g[:, :, local + first : local + first + count].rearrange("p r (c i) -> p c r i", i=4),
                minus_rowf[:].unsqueeze(1).unsqueeze(3).to_broadcast([P, count // 4, PACK, 4]),
                MULT,
            )

        def mix_piece(piece, minus_g):
            local = (piece * PIECE) % HALF
            slots = slice(piece * PIECE, (piece + 1) * PIECE)
            woven = keep.tile([P, PIECE, PACK], BF16, name="woven%d" % piece, align_bytes=64)
            steps = 1 if piece == 2 else 2
            for step in range(steps):
                weave(woven, minus_g, local, step * PIECE // steps, PIECE // steps)
            g_codes = keep.tile([P, PIECE], U32, name="g_codes%d" % piece, align_bytes=64)
            g_plane = keep.tile([P, PIECE], U8, name="g_plane%d" % piece, align_bytes=64)
            calls = 2 if piece == 0 else 1
            for call in range(calls):
                part = slice(call * PIECE // calls, (call + 1) * PIECE // calls)
                nc.vector.quantize_mx(
                    out=g_codes[:, part].bitcast(FP8X4),
                    scales=g_plane[:, part],
                    in_=woven[:, part, :].rearrange("p i r -> p (i r)"),
                )

            def mix(target, e, part=slice(0, PIECE)):
                nc.tensor.matmul_mx(
                    out=target,
                    lhsT=mix_sb[:, e * P : (e + 1) * P].bitcast(FP8X4),
                    lhsT_scale=mix_plane[:, e * P : (e + 1) * P],
                    rhs=g_codes[:, part].bitcast(FP8X4),
                    rhs_scale=g_plane[:, part],
                    start=True,
                    stop=True,
                )

            if piece == 0:
                for e, part in ((0, slice(0, LEAD)), (0, slice(LEAD, PIECE)), (1, slots)):
                    bank = psum.tile([P, BANK], F32, name="bank", tag="bank")
                    width = part.stop - part.start
                    mix(bank[:, 0:width], e, part)
                    if part.stop == LEAD:
                        nc.scalar.copy(mixed[:, e, part], bank[:, 0:width])
                    else:
                        nc.vector.tensor_copy(mixed[:, e, part], bank[:, 0:width])
            else:
                bank = psum.tile([P, BANK], F32, name="bank", tag="bank")
                for e in range(E // P):
                    mix(bank[:, e * PIECE : (e + 1) * PIECE], e)
                nc.vector.tensor_copy(
                    mixed[:, :, slots], bank[:, 0 : 2 * PIECE].rearrange("p (e i) -> p e i", e=E // P)
                )

        def post(e, first, count):
            for k, lists in enumerate((offs3_sb, offs4_sb)):
                nc.scalar.activation(
                    pages[e][k][:].indirect(listed(lists, first, count)), mixed[:, e, first : first + count], COPY
                )

        def hand_out(e):
            for c in range(Z // STORE):
                cols = slice(c * STORE, (c + 1) * STORE)
                page = keep.tile([P, STORE], F32, name="result%d%d" % (e, c))
                nc.vector.tensor_tensor(page[:], pages[e][0][:, cols], pages[e][1][:, cols], SUB)
                nc.sync.dma_start(out[e * P : (e + 1) * P, cols], page[:])

        for piece in range(2):
            mix_piece(piece, minus_g)
        w_second = keep.tile([P, PACK, HALF], F32, name="w_second", tag="q_codes3", align_bytes=64)
        minus_g_second = keep.tile([P, PACK, HALF], F32, name="minus_g1", tag="minus_g")
        for r in range(PACK):
            fetch_scaled(r, 1, w_second[:, r, :])
            fetch_less(r, 1, w_second[:, r, :], minus_g_second)
        post(0, 0, LEAD)
        post(0, LEAD, PIECE - LEAD)
        post(1, 0, PIECE)
        for e in range(E // P):
            post(e, PIECE, PIECE)
        for piece in range(2, 4):
            mix_piece(piece, minus_g_second)
            post(0, piece * PIECE, PIECE)
        hand_out(0)
        post(1, HALF, HALF)
        hand_out(1)
